import numpy as np
import ml_dtypes


def mxq(x, axis, fmt="e4m3"):
    dtype, down = {"e4m3": (ml_dtypes.float8_e4m3fn, 7), "e5m2": (ml_dtypes.float8_e5m2, 14)}[fmt]
    v = np.moveaxis(np.asarray(x, np.float32).astype(ml_dtypes.bfloat16).astype(np.float64), axis, -1)
    blocks = v.reshape(v.shape[:-1] + (-1, 32))
    amax = np.abs(blocks).max(-1, keepdims=True)
    byte = np.maximum(np.where(amax > 0, np.frexp(amax)[1] - 1 + 127, 0) - down, 1)
    scale = np.exp2(byte - 127.0)
    codes = (blocks / scale).astype(np.float32).astype(dtype).astype(np.float64)
    return np.moveaxis((codes * scale).reshape(v.shape), -1, axis)


WIDE = False


def mx_kscale(k):
    if not WIDE:
        return np.ones(k)
    levels = np.array([10, -10, 5, -5, 0])
    if k % 512:
        return np.exp2(np.random.permutation(np.resize(levels, k // 32))).repeat(32)
    a = np.empty((k // 512, 16))
    for p in range(k // 512):
        a[p, :8] = np.random.permutation(np.resize(levels, 8))
        for g in range(8):
            far = levels[np.abs(levels - a[p, g]) >= 10]
            a[p, g + 8] = far[np.random.randint(len(far))]
    return np.exp2(a.ravel()).repeat(32)


def f64(x):
    return np.asarray(x).astype(np.float64)


def striped(idx):
    return np.tile(idx.reshape(-1, 16).T, (8, 1)).astype(np.uint16)


def unstriped(offs):
    return offs[:16].T.reshape(-1).astype(np.int64)


E2M1 = np.array([0.0, 0.5, 1.0, 1.5, 2.0, 3.0, 4.0, 6.0, -0.0, -0.5, -1.0, -1.5, -2.0, -3.0, -4.0, -6.0])


def pack_weight(w, fmt):
    k, n = w.shape
    w = f64(np.asarray(w, np.float32).astype(ml_dtypes.bfloat16)).reshape(k // 32, 32, n)
    amax = np.abs(w).max(1)
    if fmt == "e4m3":
        byte = np.frexp(amax)[1] - 1 + 127 - 7
    else:
        mant, ex = np.frexp(amax / 6.0)
        byte = np.where(mant > 0.5, ex, ex - 1) + 127
    byte = np.clip(np.where(amax > 0, byte, 1), 1, 254)
    scaled = (w * np.exp2(127.0 - byte)[:, None, :]).reshape(k, n).astype(np.float32)
    by_word = np.ascontiguousarray(scaled.reshape(k // 512, 128, 4, n).transpose(0, 1, 3, 2))
    if fmt == "e4m3":
        words = by_word.astype(ml_dtypes.float8_e4m3fn).view(np.uint8)
    else:
        c = by_word.astype(ml_dtypes.float4_e2m1fn).view(np.uint8) & 0xF
        words = (c[..., 0::2] | (c[..., 1::2] << 4)).reshape(k // 512, 128, 2 * n)
    return np.ascontiguousarray(words), np.ascontiguousarray(byte.astype(np.uint8).reshape(k // 512, 16, n))


def unpack_weight(words, scales, fmt):
    g, _, n = scales.shape
    words = np.ascontiguousarray(words).reshape(g, 128, n, -1)
    if fmt == "e4m3":
        vals = words.view(ml_dtypes.float8_e4m3fn).astype(np.float64)
    else:
        nib = np.empty((g, 128, n, 4), np.uint8)
        nib[..., 0::2] = words & 0xF
        nib[..., 1::2] = words >> 4
        vals = E2M1[nib]
    vals = vals * np.repeat(np.exp2(scales.astype(np.float64) - 127.0), 8, axis=1)[..., None]
    return vals.transpose(0, 1, 3, 2).reshape(g * 512, n)


def gelu(v):
    return 0.5 * v * (1.0 + np.tanh(np.sqrt(2.0 / np.pi) * (v + 0.044715 * v**3)))


def striped8(idx):
    return np.concatenate([v.reshape(-1, 16).T for v in idx]).astype(np.uint16)


def unstriped8(offs):
    return np.stack([offs[16 * g:16 * g + 16].T.reshape(-1) for g in range(8)]).astype(np.int64)


def heads(h, wgt, idx8):
    r = np.arange(h.shape[0])
    return wgt[r // 4 % 128] * h[r[:, None], idx8[r % 512 // 64]]


def put_heads(h, wgs, idx8, t2):
    r = np.arange(h.shape[0])
    page = np.zeros((h.shape[0], t2))
    page[r[:, None], idx8[r % 512 // 64]] = wgs[r // 4 % 128] * h
    return page


K, H, N, T, S, P, T2 = 1024, 1024, 512, 2048, 1024, 512, 1024


def setup_inputs():
    n = np.random.standard_normal
    s = mx_kscale(K)[:, None]
    u = mx_kscale(H)[:, None]
    d = {}
    d["tab_words"], d["tab_scales"] = pack_weight(n((K, T)) * s, "e4m3")
    d["offs"] = striped(np.random.permutation(T)[:S])
    d["w1"] = (n((K, H)) / s / K ** 0.5).astype(np.float32)
    d["gain"] = (np.exp(0.3 * n(H)) * u[:, 0]).astype(np.float32)
    d["offs2"] = striped8(np.stack([np.random.permutation(S)[:P] for _ in range(8)]))
    d["wgt"] = np.repeat(np.random.uniform(0.5, 2.0, (8, P)), 16, axis=0).astype(np.float32)
    d["context"] = (n((H, P)) * u).astype(np.float32)
    d["wa_words"], d["wa_scales"] = pack_weight(0.8 * n((H, N)) / u / H ** 0.5, "e2m1")
    d["wb"] = (0.8 * n((H, N)) / u / H ** 0.5).astype(np.float32)
    d["offs3"] = striped8(np.stack([np.random.permutation(T2)[:P] for _ in range(8)]))
    d["wgo"] = np.repeat(np.random.uniform(0.5, 2.0, (8, P)), 16, axis=0).astype(np.float32)
    return d


def reference(tab_words, tab_scales, offs, w1, gain, offs2, wgt, context, wa_words, wa_scales, wb, offs3, wgo):
    v = unpack_weight(tab_words, tab_scales, "e4m3")[:, unstriped(offs)]
    h = f64(gain)[:, None] * (mxq(f64(w1), 0, "e4m3").T @ v)
    x = heads(h, f64(wgt), unstriped8(offs2))
    zq = mxq(x + f64(context), 0, "e4m3")
    first = unpack_weight(wa_words, wa_scales, "e2m1").T @ zq
    second = mxq(f64(wb), 0, "e4m3").T @ zq
    y = np.square(first - second) / (1.0 + np.abs(first))
    return put_heads(y, f64(wgo), unstriped8(offs3), T2)

@@ -1,0 +1,290 @@
+from contextlib import ExitStack
+
+import concourse.mybir as mybir
+from concourse.masks import make_identity
+
+K, H, N, T, S, M, T2 = 1024, 1024, 512, 2048, 1024, 512, 1024
+FLOPS = 2 * K * H * S + 2 * 2 * H * N * M
+
+F32 = mybir.dt.float32
+BF16 = mybir.dt.bfloat16
+I32 = mybir.dt.int32
+U32 = mybir.dt.uint32
+U16 = mybir.dt.uint16
+U8 = mybir.dt.uint8
+FP8X4 = mybir.dt.float8_e4m3fn_x4
+FP4X4 = mybir.dt.float4_e2m1fn_x4
+ACT = mybir.ActivationFunctionType
+ALU = mybir.AluOpType
+
+P = 128
+PACK = 4
+KP = P * PACK
+BANK = 512
+LIST = 16
+
+
+def tile_list_panel_disagreement_features_kernel(
+    tc, tab_words, tab_scales, offs, w1, gain, offs2, wgt, context, wa_words, wa_scales, wb, offs3, wgo, out
+):
+    nc = tc.nc
+    with ExitStack() as ctx:
+        keep = ctx.enter_context(tc.tile_pool(name="keep", bufs=1))
+        ring = ctx.enter_context(tc.tile_pool(name="ring", bufs=1))
+        psum = ctx.enter_context(tc.psum_pool(name="psum", bufs=1))
+
+        list1 = keep.tile([P, S // LIST], U16, name="list1")
+        list2 = keep.tile([P, M // LIST], U16, name="list2")
+        list3 = keep.tile([P, M // LIST], U16, name="list3")
+
+        tab_sc = keep.tile([P, T], U8, name="tab_sc", align_bytes=64)
+        nc.gpsimd.memset(tab_sc[:].bitcast(I32), 0)
+        wa_sc = keep.tile([P, 2, N], U8, name="wa_sc", align_bytes=64)
+        nc.vector.memset(wa_sc[:].rearrange("p a c -> p (a c)").bitcast(I32), 0)
+        pages = [keep.tile([P, T2], F32, name=f"page{i}") for i in range(PACK)]
+        for page in pages:
+            nc.vector.memset(page[:], 0.0)
+        ident = keep.tile([P, P], F32, name="ident")
+        make_identity(nc, ident[:])
+
+        def load_rows(src, name, cuts=(0, PACK)):
+            raw = ring.tile([P, PACK, BANK], F32, name=name, tag="raw", bufs=4)
+            rows = src.rearrange("(p j) c -> p j c", j=PACK)
+            for j0, j1 in zip(cuts, cuts[1:]):
+                nc.sync.dma_start(out=raw[:, j0:j1, :], in_=rows[:, j0:j1, :])
+            return raw
+
+        def load_table(a, pieces=1):
+            words = keep.tile([P, T], I32, name=f"tab_w{a}", align_bytes=64)
+            src = tab_words[a].rearrange("p t i -> p (t i)").bitcast(I32)
+            step = T // pieces
+            for c in range(0, T, step):
+                nc.sync.dma_start(out=words[:, c : c + step], in_=src[:, c : c + step])
+            return words
+
+        def load_context(b):
+            rows = keep.tile([P, PACK, M], F32, name=f"ctx{b}")
+            nc.sync.dma_start(out=rows[:], in_=context[b * KP : (b + 1) * KP, :].rearrange("(p t) m -> p t m", t=PACK))
+            return rows
+
+        nc.sync.dma_start(out=list1[:], in_=offs)
+        gains = keep.tile([P, 2, PACK], F32, name="gains")
+        nc.sync.dma_start(out=gains[:], in_=gain.rearrange("(b p t) -> p b t", b=2, t=PACK))
+        nc.sync.dma_start(out=list2[:], in_=offs2)
+        nc.sync.dma_start(out=list3[:], in_=offs3)
+        tab_w = [load_table(0, 2)]
+        for q in range(4):
+            nc.sync.dma_start(
+                out=tab_sc[32 * q : 32 * q + 8, :].bitcast(I32),
+                in_=tab_scales[:, 4 * q : 4 * q + 4, :].bitcast(I32),
+            )
+        w1_raw = {(0, 0): load_rows(w1[0:KP, 0:KP], "w1_raw00", (0, 1, 2, 4))}
+        tab_w.append(load_table(1))
+        w1_raw[1, 0] = load_rows(w1[KP : 2 * KP, 0:KP], "w1_raw10")
+        wgt_sb = keep.tile([P, M], F32, name="wgt_sb")
+        nc.sync.dma_start(out=wgt_sb[:], in_=wgt)
+        w1_raw[0, 1] = load_rows(w1[0:KP, KP : 2 * KP], "w1_raw01")
+        w1_raw[1, 1] = load_rows(w1[KP : 2 * KP, KP : 2 * KP], "w1_raw11")
+        ctx_sb = [load_context(0)]
+        wb_raw = [load_rows(wb[b * KP : (b + 1) * KP, :], f"wb_raw{b}") for b in range(2)]
+        ctx_sb.append(load_context(1))
+        wa_w = keep.tile([P, 2, 2 * N], U8, name="wa_w", align_bytes=64)
+        nc.sync.dma_start(out=wa_w[:].bitcast(I32), in_=wa_words.rearrange("a p c -> p a c").bitcast(I32))
+        for q in range(4):
+            nc.sync.dma_start(
+                out=wa_sc[32 * q : 32 * q + 4].bitcast(I32),
+                in_=wa_scales[:, 4 * q : 4 * q + 4, :].rearrange("a r c -> r a c").bitcast(I32),
+            )
+        wgo_sb = keep.tile([P, M], F32, name="wgo_sb")
+        nc.sync.dma_start(out=wgo_sb[:], in_=wgo)
+
+        v_w = [keep.tile([P, S], U32, name="v_w0", align_bytes=64)]
+        v_sc = keep.tile([P, S], U8, name="v_sc", align_bytes=64)
+        nc.vector.tensor_copy(v_w[0][:], tab_w[0][:].bitcast(U32).indirect(list1[:]))
+        nc.vector.tensor_copy(v_sc[:], tab_sc[:].indirect(list1[:]))
+
+        def cast(on_vector, dst, src):
+            if on_vector:
+                nc.vector.tensor_copy(dst, src)
+            else:
+                nc.scalar.copy(dst, src)
+
+        def quantize(grouped, name):
+            width = grouped.shape[1] // PACK
+            codes = keep.tile([P, width], U32, name=name + "_w", tag=name, align_bytes=64)
+            scales = keep.tile([P, width], U8, name=name + "_sc", align_bytes=64)
+            nc.vector.quantize_mx(out=codes[:].bitcast(FP8X4), scales=scales[:], in_=grouped[:])
+            return codes, scales
+
+        def group_w1(a, b, u, on_vector):
+            tag = f"w1g{a}{u}" if b == 0 else f"h0{2 * u + a}"
+            grouped = keep.tile([P, 2 * KP], BF16, name=f"w1g{a}{b}{u}", tag=tag, align_bytes=64)
+            cast(
+                on_vector,
+                grouped[:].rearrange("p (e m j) -> p m j e", e=2, j=PACK),
+                w1_raw[a, b][:].rearrange("p j (m t) -> p m j t", t=PACK)[:, :, :, 2 * u : 2 * u + 2],
+            )
+            return grouped
+
+        def group_wb(b, u, on_vector):
+            tag = f"h0{u}" if b == 0 else f"w1q{u}11"
+            grouped = keep.tile([P, 2 * KP], BF16, name=f"wbg{b}{u}", tag=tag, align_bytes=64)
+            cast(
+                on_vector,
+                grouped[:].rearrange("p (c i j) -> p c j i", i=4, j=PACK),
+                wb_raw[b][:, :, 256 * u : 256 * (u + 1)].rearrange("p j (c i) -> p c j i", i=4),
+            )
+            return grouped
+
+        w1_q = {}
+
+        def first_pass(a, b, t, half, bank):
+            codes, scales = w1_q[a, b, t // 2]
+            cols = slice((t % 2) * P, (t % 2 + 1) * P)
+            picked = slice(half * BANK, (half + 1) * BANK)
+            nc.tensor.matmul_mx(
+                out=bank[:],
+                lhsT=codes[:, cols].bitcast(FP8X4),
+                lhsT_scale=scales[:, cols],
+                rhs=v_w[a][:, picked].bitcast(FP8X4),
+                rhs_scale=v_sc[4 * a :, picked],
+                start=(a == 0),
+                stop=(a == 1),
+            )
+
+        def new_bank(name, number):
+            return psum.tile([P, BANK], F32, name=name, tag=f"bank{number}")
+
+        def leave_h(b, t, banks):
+            h = keep.tile([P, S], F32, name=f"h{b}{t}", tag=f"h{b}{t}", align_bytes=64)
+            for half in range(2):
+                nc.scalar.activation(
+                    out=h[:, half * BANK : (half + 1) * BANK],
+                    in_=banks[half][:],
+                    func=ACT.Copy,
+                    scale=gains[:, b, t : t + 1],
+                )
+            return h
+
+        def pick(h, x, lo, hi):
+            nc.vector.tensor_tensor(
+                x, h[:].indirect(list2[:, lo // LIST : hi // LIST]), wgt_sb[:, lo:hi], ALU.mult
+            )
+
+        def add_context(b, x, lo, hi, tag):
+            z = ring.tile([P, (hi - lo) * PACK], BF16, name=f"z{b}{lo}", tag=tag, align_bytes=64)
+            nc.vector.tensor_tensor(
+                z[:].rearrange("p (c i t) -> p c t i", i=4, t=PACK),
+                x.rearrange("p t (c i) -> p c t i", i=4),
+                ctx_sb[b][:, :, lo:hi].rearrange("p t (c i) -> p c t i", i=4),
+                ALU.add,
+            )
+            return z
+
+        for u in range(2):
+            w1_q[0, 0, u] = quantize(group_w1(0, 0, u, False), f"w1q00{u}")
+        banks = {(t, half): new_bank(f"h0{t}{half}", 2 * t + half) for t in range(PACK) for half in range(2)}
+        for t in range(PACK):
+            for half in range(2):
+                first_pass(0, 0, t, half, banks[t, half])
+        v_w.append(keep.tile([P, S], U32, name="v_w1", tag="w1g01", align_bytes=64))
+        nc.vector.tensor_copy(v_w[1][:], tab_w[1][:].bitcast(U32).indirect(list1[:]))
+        for u in range(2):
+            w1_q[1, 0, u] = quantize(group_w1(1, 0, u, u == 0), f"w1q10{u}")
+        x0 = ring.tile([P, PACK, M], F32, name="x0")
+        for t in range(PACK):
+            for half in range(2):
+                first_pass(1, 0, t, half, banks[t, half])
+            pick(leave_h(0, t, [banks[t, 0], banks[t, 1]]), x0[:, t, :], 0, M)
+            if t % 2 == 1:
+                for a in range(2):
+                    w1_q[a, 1, t // 2] = quantize(group_w1(a, 1, t // 2, t == 1 and a == 1), f"w1q{a}1{t // 2}")
+
+        z_q = {}
+        h1 = []
+        x1 = ring.tile([P, PACK, P], F32, name="x1_0", tag="x1")
+        for t in range(PACK):
+            pair = [new_bank(f"h1{t}{half}", 2 * t + half) for half in range(2)]
+            for half in range(2):
+                for a in range(2):
+                    first_pass(a, 1, t, half, pair[half])
+            h1.append(leave_h(1, t, pair))
+            pick(h1[t], x1[:, t, :], 0, P)
+        z_q[0, 0] = quantize(add_context(0, x0[:, :, 0 : 2 * P], 0, 2 * P, "za"), "zq00")
+
+        wb_w = [keep.tile([P, N], U32, name=f"wb_w{b}", align_bytes=64) for b in range(2)]
+        wb_sc = [keep.tile([P, N], U8, name=f"wb_sc{b}", align_bytes=64) for b in range(2)]
+        for b in range(2):
+            for u in range(2):
+                grouped = group_wb(b, u, u == 1)
+                cols = slice(256 * u, 256 * (u + 1))
+                nc.vector.quantize_mx(out=wb_w[b][:, cols].bitcast(FP8X4), scales=wb_sc[b][:, cols], in_=grouped[:])
+
+        z_q[1, 0] = quantize(add_context(1, x1[:], 0, P, "zb"), "zq10")
+        for lo, hi in ((P, 2 * P), (2 * P, M)):
+            x1 = ring.tile([P, PACK, hi - lo], F32, name=f"x1_{lo}", tag="x1")
+            for t in range(PACK):
+                pick(h1[t], x1[:, t, :], lo, hi)
+            z_q[1, lo] = quantize(add_context(1, x1[:], lo, hi, "zc" if lo == P else "zb"), f"zq1{lo}")
+        z_q[0, 2 * P] = quantize(add_context(0, x0[:, :, 2 * P : M], 2 * P, M, "zc"), "zq02")
+
+        def z_columns(b, lo):
+            start = max(s for bb, s in z_q if bb == b and s <= lo)
+            codes, scales = z_q[b, start]
+            cols = slice(lo - start, lo - start + P)
+            return codes[:, cols].bitcast(FP8X4), scales[:, cols]
+
+        def second_stage(c, banks):
+            lo = c * P
+            first_t, second_t = new_bank(f"ft{c}", banks[0]), new_bank(f"st{c}", banks[1])
+            for b in range(2):
+                codes, scales = z_columns(b, lo)
+                nc.tensor.matmul_mx(
+                    out=first_t[:], lhsT=codes, lhsT_scale=scales,
+                    rhs=wa_w[:, b, :].bitcast(FP4X4), rhs_scale=wa_sc[:, b, :],
+                    start=(b == 0), stop=(b == 1),
+                )
+                nc.tensor.matmul_mx(
+                    out=second_t[:], lhsT=codes, lhsT_scale=scales,
+                    rhs=wb_w[b][:].bitcast(FP8X4), rhs_scale=wb_sc[b][:],
+                    start=(b == 0), stop=(b == 1),
+                )
+            f_sb, s_sb, size, root, damp, square, y = [
+                ring.tile([P, BANK], F32, name=f"{tag}{c}", tag=tag, bufs=2)
+                for tag in ("f_sb", "s_sb", "size", "root", "damp", "square", "y")
+            ]
+            nc.scalar.copy(
+                f_sb[:].rearrange("m (i p) -> m i p", i=PACK), first_t[:].rearrange("m (p i) -> m i p", i=PACK)
+            )
+            nc.scalar.activation(
+                out=s_sb[:].rearrange("m (i p) -> m i p", i=PACK),
+                in_=second_t[:].rearrange("m (p i) -> m i p", i=PACK),
+                func=ACT.Copy,
+                scale=-1.0,
+            )
+            diff, damp_t = new_bank(f"d{c}", banks[2]), new_bank(f"r{c}", banks[3])
+            for i in range(PACK):
+                cols = slice(i * P, (i + 1) * P)
+                nc.tensor.matmul(diff[:, cols], f_sb[:, cols], ident[:], start=True, stop=False, is_transpose=True)
+                nc.tensor.matmul(diff[:, cols], s_sb[:, cols], ident[:], start=False, stop=True, is_transpose=True)
+            nc.scalar.activation(out=size[:], in_=f_sb[:], func=ACT.Abs)
+            nc.scalar.activation(out=root[:], in_=size[:], func=ACT.Abs_reciprocal_sqrt, bias=1.0)
+            nc.scalar.activation(out=square[:], in_=diff[:], func=ACT.Square)
+            nc.scalar.activation(out=damp[:], in_=root[:], func=ACT.Square)
+            for i in range(PACK):
+                cols = slice(i * P, (i + 1) * P)
+                nc.tensor.transpose(damp_t[:, cols], damp[:, cols], ident[:])
+            nc.vector.tensor_tensor(y[:], square[:], damp_t[:], ALU.mult)
+            for i in range(PACK):
+                nc.vector.tensor_tensor(
+                    pages[i][:].indirect(list3[:, lo // LIST : (lo + P) // LIST]),
+                    y[:, i * P : (i + 1) * P],
+                    wgo_sb[:, lo : lo + P],
+                    ALU.mult,
+                )
+
+        for c, banks in enumerate([(0, 1, 2, 3), (1, 2, 0, 4), (2, 0, 1, 5), (0, 1, 2, 6)]):
+            second_stage(c, banks)
+        out_rows = out.rearrange("(p i) c -> p i c", i=PACK)
+        for i in range(PACK):
+            nc.sync.dma_start(out=out_rows[:, i, :], in_=pages[i][:])

@@ -1,7 +1,6 @@
 from contextlib import ExitStack
 
 import concourse.mybir as mybir
-from concourse.masks import make_identity
 
 K, H, N, T, S, M, T2 = 1024, 1024, 512, 2048, 1024, 512, 1024
 FLOPS = 2 * K * H * S + 2 * 2 * H * N * M
@@ -40,12 +39,10 @@ def tile_list_panel_disagreement_features_kernel(
         tab_sc = keep.tile([P, T], U8, name="tab_sc", align_bytes=64)
         nc.gpsimd.memset(tab_sc[:].bitcast(I32), 0)
         wa_sc = keep.tile([P, 2, N], U8, name="wa_sc", align_bytes=64)
-        nc.vector.memset(wa_sc[:].rearrange("p a c -> p (a c)").bitcast(I32), 0)
+        nc.gpsimd.memset(wa_sc[:].rearrange("p a c -> p (a c)").bitcast(I32), 0)
         pages = [keep.tile([P, T2], F32, name=f"page{i}") for i in range(PACK)]
         for page in pages:
             nc.vector.memset(page[:], 0.0)
-        ident = keep.tile([P, P], F32, name="ident")
-        make_identity(nc, ident[:])
 
         def load_rows(src, name, cuts=(0, PACK)):
             raw = ring.tile([P, PACK, BANK], F32, name=name, tag="raw", bufs=4)
@@ -81,13 +78,6 @@ def tile_list_panel_disagreement_features_kernel(
         w1_raw = {(0, 0): load_rows(w1[0:KP, 0:KP], "w1_raw00", (0, 1, 2, 4))}
         tab_w.append(load_table(1))
         w1_raw[1, 0] = load_rows(w1[KP : 2 * KP, 0:KP], "w1_raw10")
-        wgt_sb = keep.tile([P, M], F32, name="wgt_sb")
-        nc.sync.dma_start(out=wgt_sb[:], in_=wgt)
-        w1_raw[0, 1] = load_rows(w1[0:KP, KP : 2 * KP], "w1_raw01")
-        w1_raw[1, 1] = load_rows(w1[KP : 2 * KP, KP : 2 * KP], "w1_raw11")
-        ctx_sb = [load_context(0)]
-        wb_raw = [load_rows(wb[b * KP : (b + 1) * KP, :], f"wb_raw{b}") for b in range(2)]
-        ctx_sb.append(load_context(1))
         wa_w = keep.tile([P, 2, 2 * N], U8, name="wa_w", align_bytes=64)
         nc.sync.dma_start(out=wa_w[:].bitcast(I32), in_=wa_words.rearrange("a p c -> p a c").bitcast(I32))
         for q in range(4):
@@ -95,6 +85,13 @@ def tile_list_panel_disagreement_features_kernel(
                 out=wa_sc[32 * q : 32 * q + 4].bitcast(I32),
                 in_=wa_scales[:, 4 * q : 4 * q + 4, :].rearrange("a r c -> r a c").bitcast(I32),
             )
+        wgt_sb = keep.tile([P, M], F32, name="wgt_sb")
+        nc.sync.dma_start(out=wgt_sb[:], in_=wgt)
+        w1_raw[0, 1] = load_rows(w1[0:KP, KP : 2 * KP], "w1_raw01")
+        w1_raw[1, 1] = load_rows(w1[KP : 2 * KP, KP : 2 * KP], "w1_raw11")
+        ctx_sb = [load_context(0)]
+        wb_raw = [load_rows(wb[b * KP : (b + 1) * KP, :], f"wb_raw{b}") for b in range(2)]
+        ctx_sb.append(load_context(1))
         wgo_sb = keep.tile([P, M], F32, name="wgo_sb")
         nc.sync.dma_start(out=wgo_sb[:], in_=wgo)
 
@@ -113,7 +110,7 @@ def tile_list_panel_disagreement_features_kernel(
             width = grouped.shape[1] // PACK
             codes = keep.tile([P, width], U32, name=name + "_w", tag=name, align_bytes=64)
             scales = keep.tile([P, width], U8, name=name + "_sc", align_bytes=64)
-            nc.vector.quantize_mx(out=codes[:].bitcast(FP8X4), scales=scales[:], in_=grouped[:])
+            nc.vector.quantize_mx(out=codes[:].bitcast(FP8X4), scales=scales[:], in_=grouped)
             return codes, scales
 
         def group_w1(a, b, u, on_vector):
@@ -124,15 +121,14 @@ def tile_list_panel_disagreement_features_kernel(
                 grouped[:].rearrange("p (e m j) -> p m j e", e=2, j=PACK),
                 w1_raw[a, b][:].rearrange("p j (m t) -> p m j t", t=PACK)[:, :, :, 2 * u : 2 * u + 2],
             )
-            return grouped
+            return grouped[:]
 
-        def group_wb(b, u, on_vector):
-            tag = f"h0{u}" if b == 0 else f"w1q{u}11"
-            grouped = keep.tile([P, 2 * KP], BF16, name=f"wbg{b}{u}", tag=tag, align_bytes=64)
-            cast(
-                on_vector,
-                grouped[:].rearrange("p (c i j) -> p c j i", i=4, j=PACK),
-                wb_raw[b][:, :, 256 * u : 256 * (u + 1)].rearrange("p j (c i) -> p c j i", i=4),
+        def group_wb(b, u, grouped):
+            nc.scalar.activation(
+                out=grouped.rearrange("p (e m j) -> p m j e", e=2, j=PACK),
+                in_=wb_raw[b][:].rearrange("p j (m t) -> p m j t", t=PACK)[:, :, :, 2 * u : 2 * u + 2],
+                func=ACT.Copy,
+                scale=-1.0 if u == 0 else 1.0,
             )
             return grouped
 
@@ -157,13 +153,13 @@ def tile_list_panel_disagreement_features_kernel(
 
         def leave_h(b, t, banks):
             h = keep.tile([P, S], F32, name=f"h{b}{t}", tag=f"h{b}{t}", align_bytes=64)
+            row_gain = gains[:, b, t : t + 1]
             for half in range(2):
-                nc.scalar.activation(
-                    out=h[:, half * BANK : (half + 1) * BANK],
-                    in_=banks[half][:],
-                    func=ACT.Copy,
-                    scale=gains[:, b, t : t + 1],
-                )
+                cols = slice(half * BANK, (half + 1) * BANK)
+                if (b, t, half) == (0, 0, 1):
+                    nc.vector.tensor_scalar(h[:, cols], banks[half][:], row_gain, None, ALU.mult)
+                else:
+                    nc.scalar.activation(out=h[:, cols], in_=banks[half][:], func=ACT.Copy, scale=row_gain)
             return h
 
         def pick(h, x, lo, hi):
@@ -174,12 +170,12 @@ def tile_list_panel_disagreement_features_kernel(
         def add_context(b, x, lo, hi, tag):
             z = ring.tile([P, (hi - lo) * PACK], BF16, name=f"z{b}{lo}", tag=tag, align_bytes=64)
             nc.vector.tensor_tensor(
-                z[:].rearrange("p (c i t) -> p c t i", i=4, t=PACK),
-                x.rearrange("p t (c i) -> p c t i", i=4),
-                ctx_sb[b][:, :, lo:hi].rearrange("p t (c i) -> p c t i", i=4),
+                z[:].rearrange("p (c i t) -> p c t i", i=2, t=PACK),
+                x.rearrange("p t (c i) -> p c t i", i=2),
+                ctx_sb[b][:, :, lo:hi].rearrange("p t (c i) -> p c t i", i=2),
                 ALU.add,
             )
-            return z
+            return z[:]
 
         for u in range(2):
             w1_q[0, 0, u] = quantize(group_w1(0, 0, u, False), f"w1q00{u}")
@@ -191,6 +187,8 @@ def tile_list_panel_disagreement_features_kernel(
         nc.vector.tensor_copy(v_w[1][:], tab_w[1][:].bitcast(U32).indirect(list1[:]))
         for u in range(2):
             w1_q[1, 0, u] = quantize(group_w1(1, 0, u, u == 0), f"w1q10{u}")
+        wa_pw = keep.tile([P, 2, N], U16, name="wa_pw", tag="w1g10", align_bytes=64)
+        wa_psc = keep.tile([P, 2, N], U8, name="wa_psc", tag="w1g11", align_bytes=64)
         x0 = ring.tile([P, PACK, M], F32, name="x0")
         for t in range(PACK):
             for half in range(2):
@@ -199,92 +197,116 @@ def tile_list_panel_disagreement_features_kernel(
             if t % 2 == 1:
                 for a in range(2):
                     w1_q[a, 1, t // 2] = quantize(group_w1(a, 1, t // 2, t == 1 and a == 1), f"w1q{a}1{t // 2}")
+        nc.vector.tensor_copy(
+            wa_pw[:].rearrange("p a (i m) -> p a i m", i=PACK),
+            wa_w[:].bitcast(U16).rearrange("p a (m i) -> p a i m", i=PACK),
+        )
+        nc.vector.tensor_copy(
+            wa_psc[:].rearrange("p a (i m) -> p a i m", i=PACK),
+            wa_sc[:].rearrange("p a (m i) -> p a i m", i=PACK),
+        )
 
+        half_m = M // 2
         z_q = {}
-        h1 = []
-        x1 = ring.tile([P, PACK, P], F32, name="x1_0", tag="x1")
+        wb_q = {}
+        x1 = ring.tile([P, PACK, M], F32, name="x1")
         for t in range(PACK):
             pair = [new_bank(f"h1{t}{half}", 2 * t + half) for half in range(2)]
             for half in range(2):
                 for a in range(2):
                     first_pass(a, 1, t, half, pair[half])
-            h1.append(leave_h(1, t, pair))
-            pick(h1[t], x1[:, t, :], 0, P)
-        z_q[0, 0] = quantize(add_context(0, x0[:, :, 0 : 2 * P], 0, 2 * P, "za"), "zq00")
-
-        wb_w = [keep.tile([P, N], U32, name=f"wb_w{b}", align_bytes=64) for b in range(2)]
-        wb_sc = [keep.tile([P, N], U8, name=f"wb_sc{b}", align_bytes=64) for b in range(2)]
+            h = leave_h(1, t, pair)
+            if t < PACK - 1:
+                pick(h, x1[:, t, :], 0, M)
+            else:
+                pick(h, x1[:, t, 0:half_m], 0, half_m)
+            if t == 0:
+                z_q[0, 0] = quantize(add_context(0, x0[:], 0, M, "za"), "zq0")
+            if t < 2:
+                tag = "h00" if t == 0 else "w1q010"
+                grouped = keep.tile([P, 2 * KP], BF16, name=f"wbg{t}0", tag=tag, align_bytes=64)
+                wb_q[t, 0] = quantize(group_wb(t, 0, grouped[:]), f"wbq{t}0")
+        z_q[1, 0] = quantize(add_context(1, x1[:, :, 0:half_m], 0, half_m, "zb"), "zq10")
+        pick(h, x1[:, PACK - 1, half_m:M], half_m, M)
+        z_q[1, half_m] = quantize(add_context(1, x1[:, :, half_m:M], half_m, M, "zc"), "zq11")
+        grouped = keep.tile([P, 2, 2 * KP], BF16, name="wbg1", tag="h12", align_bytes=64)
         for b in range(2):
-            for u in range(2):
-                grouped = group_wb(b, u, u == 1)
-                cols = slice(256 * u, 256 * (u + 1))
-                nc.vector.quantize_mx(out=wb_w[b][:, cols].bitcast(FP8X4), scales=wb_sc[b][:, cols], in_=grouped[:])
+            wb_q[b, 1] = quantize(group_wb(b, 1, grouped[:, b, :]), f"wbq{b}1")
 
-        z_q[1, 0] = quantize(add_context(1, x1[:], 0, P, "zb"), "zq10")
-        for lo, hi in ((P, 2 * P), (2 * P, M)):
-            x1 = ring.tile([P, PACK, hi - lo], F32, name=f"x1_{lo}", tag="x1")
-            for t in range(PACK):
-                pick(h1[t], x1[:, t, :], lo, hi)
-            z_q[1, lo] = quantize(add_context(1, x1[:], lo, hi, "zc" if lo == P else "zb"), f"zq1{lo}")
-        z_q[0, 2 * P] = quantize(add_context(0, x0[:, :, 2 * P : M], 2 * P, M, "zc"), "zq02")
-
-        def z_columns(b, lo):
-            start = max(s for bb, s in z_q if bb == b and s <= lo)
-            codes, scales = z_q[b, start]
-            cols = slice(lo - start, lo - start + P)
-            return codes[:, cols].bitcast(FP8X4), scales[:, cols]
-
-        def second_stage(c, banks):
-            lo = c * P
-            first_t, second_t = new_bank(f"ft{c}", banks[0]), new_bank(f"st{c}", banks[1])
-            for b in range(2):
-                codes, scales = z_columns(b, lo)
+        def second_pass(sums, weight, b, i, lo, hi, start, stop):
+            cols = slice(i * P, (i + 1) * P)
+            if weight == "a":
+                lhs, lhs_scale = wa_pw[:, b, cols].bitcast(FP4X4), wa_psc[:, b, cols]
+            else:
+                codes, scales = wb_q[b, i // 2]
+                cols = slice((i % 2) * P, (i % 2 + 1) * P)
+                lhs, lhs_scale = codes[:, cols].bitcast(FP8X4), scales[:, cols]
+            pieces = [(lo, hi)] if b == 0 else [(s, s + half_m) for s in range(lo, hi, half_m)]
+            for n, (c0, c1) in enumerate(pieces):
+                base = 0 if b == 0 else c0
+                codes, scales = z_q[b, base]
                 nc.tensor.matmul_mx(
-                    out=first_t[:], lhsT=codes, lhsT_scale=scales,
-                    rhs=wa_w[:, b, :].bitcast(FP4X4), rhs_scale=wa_sc[:, b, :],
-                    start=(b == 0), stop=(b == 1),
-                )
-                nc.tensor.matmul_mx(
-                    out=second_t[:], lhsT=codes, lhsT_scale=scales,
-                    rhs=wb_w[b][:].bitcast(FP8X4), rhs_scale=wb_sc[b][:],
-                    start=(b == 0), stop=(b == 1),
-                )
-            f_sb, s_sb, size, root, damp, square, y = [
-                ring.tile([P, BANK], F32, name=f"{tag}{c}", tag=tag, bufs=2)
-                for tag in ("f_sb", "s_sb", "size", "root", "damp", "square", "y")
-            ]
-            nc.scalar.copy(
-                f_sb[:].rearrange("m (i p) -> m i p", i=PACK), first_t[:].rearrange("m (p i) -> m i p", i=PACK)
-            )
-            nc.scalar.activation(
-                out=s_sb[:].rearrange("m (i p) -> m i p", i=PACK),
-                in_=second_t[:].rearrange("m (p i) -> m i p", i=PACK),
-                func=ACT.Copy,
-                scale=-1.0,
-            )
-            diff, damp_t = new_bank(f"d{c}", banks[2]), new_bank(f"r{c}", banks[3])
-            for i in range(PACK):
-                cols = slice(i * P, (i + 1) * P)
-                nc.tensor.matmul(diff[:, cols], f_sb[:, cols], ident[:], start=True, stop=False, is_transpose=True)
-                nc.tensor.matmul(diff[:, cols], s_sb[:, cols], ident[:], start=False, stop=True, is_transpose=True)
-            nc.scalar.activation(out=size[:], in_=f_sb[:], func=ACT.Abs)
-            nc.scalar.activation(out=root[:], in_=size[:], func=ACT.Abs_reciprocal_sqrt, bias=1.0)
-            nc.scalar.activation(out=square[:], in_=diff[:], func=ACT.Square)
-            nc.scalar.activation(out=damp[:], in_=root[:], func=ACT.Square)
-            for i in range(PACK):
-                cols = slice(i * P, (i + 1) * P)
-                nc.tensor.transpose(damp_t[:, cols], damp[:, cols], ident[:])
-            nc.vector.tensor_tensor(y[:], square[:], damp_t[:], ALU.mult)
-            for i in range(PACK):
-                nc.vector.tensor_tensor(
-                    pages[i][:].indirect(list3[:, lo // LIST : (lo + P) // LIST]),
-                    y[:, i * P : (i + 1) * P],
-                    wgo_sb[:, lo : lo + P],
-                    ALU.mult,
+                    out=sums[:, c0 - lo : c1 - lo], lhsT=lhs, lhsT_scale=lhs_scale,
+                    rhs=codes[:, c0 - base : c1 - base].bitcast(FP8X4), rhs_scale=scales[:, c0 - base : c1 - base],
+                    start=start and n == 0, stop=stop and n == len(pieces) - 1,
                 )
 
-        for c, banks in enumerate([(0, 1, 2, 3), (1, 2, 0, 4), (2, 0, 1, 5), (0, 1, 2, 6)]):
-            second_stage(c, banks)
+        def work_tile(tag, name, width):
+            return ring.tile([P, width], F32, name=f"{tag}{name}", tag=tag, bufs=2)[:]
+
+        def root_of(first, name, width):
+            size, root = work_tile("size", name, width), work_tile("root", name, width)
+            nc.scalar.activation(out=size, in_=first, func=ACT.Abs)
+            nc.scalar.activation(out=root, in_=size, func=ACT.Abs_reciprocal_sqrt, bias=1.0)
+            return root
+
         out_rows = out.rearrange("(p i) c -> p i c", i=PACK)
-        for i in range(PACK):
-            nc.sync.dma_start(out=out_rows[:, i, :], in_=pages[i][:])
+
+        def put(i, y, lo, hi):
+            nc.vector.tensor_tensor(
+                pages[i][:].indirect(list3[:, lo // LIST : hi // LIST]), y, wgo_sb[:, lo:hi], ALU.mult
+            )
+            if hi == M:
+                nc.sync.dma_start(out=out_rows[:, i, :], in_=pages[i][:])
+
+        def finish_summed(i, first, diff, lo, hi):
+            name, width = f"{i}_{lo}", hi - lo
+            root = root_of(first, name, width)
+            damp, square, y = (work_tile(tag, name, width) for tag in ("damp", "square", "y"))
+            nc.scalar.activation(out=damp, in_=root, func=ACT.Square)
+            nc.scalar.activation(out=square, in_=diff, func=ACT.Square)
+            nc.vector.tensor_tensor(y, square, damp, ALU.mult)
+            put(i, y, lo, hi)
+
+        for half in range(2):
+            lo, hi = half * half_m, (half + 1) * half_m
+            bank = new_bank(f"o0{half}", half)
+            first, diff = bank[:, 0:half_m], bank[:, half_m:M]
+            for b in range(2):
+                second_pass(first, "a", b, 0, lo, hi, b == 0, False)
+                second_pass(diff, "a", b, 0, lo, hi, False, False)
+                second_pass(diff, "b", b, 0, lo, hi, False, b == 1)
+            finish_summed(0, first, diff, lo, hi)
+
+        first, diff = new_bank("o1f", 2)[:], new_bank("o1d", 3)[:]
+        for b in range(2):
+            second_pass(first, "a", b, 1, 0, M, b == 0, b == 1)
+            second_pass(diff, "a", b, 1, 0, M, b == 0, False)
+            second_pass(diff, "b", b, 1, 0, M, False, b == 1)
+        finish_summed(1, first, diff, 0, M)
+
+        rel = {}
+        for i in (2, 3):
+            first, second = new_bank(f"o{i}f", 2 * i)[:], new_bank(f"o{i}s", 2 * i + 1)[:]
+            for b in range(2):
+                second_pass(second, "b", b, i, 0, M, b == 0, b == 1)
+                second_pass(first, "a", b, i, 0, M, b == 0, b == 1)
+            second_sb, diff, rel[i] = (work_tile(tag, i, M) for tag in ("second", "diff", "rel"))
+            nc.scalar.copy(second_sb, second)
+            root = root_of(first, i, M)
+            nc.vector.tensor_tensor(diff, first, second_sb, ALU.subtract)
+            nc.vector.tensor_tensor(rel[i], diff, root, ALU.mult)
+        for i in (2, 3):
+            y = work_tile("y", i, M)
+            nc.scalar.activation(out=y, in_=rel[i], func=ACT.Square)
+            put(i, y, 0, M)

@@ -67,6 +67,8 @@ def tile_list_panel_disagreement_features_kernel(
         nc.sync.dma_start(out=list1[:], in_=offs)
         gains = keep.tile([P, 2, PACK], F32, name="gains")
         nc.sync.dma_start(out=gains[:], in_=gain.rearrange("(b p t) -> p b t", b=2, t=PACK))
+        warm = keep.tile([P, 1], F32, name="warm")
+        nc.scalar.activation(out=warm[:], in_=gains[:, 0, 0:1], func=ACT.Abs_reciprocal_sqrt, bias=1.0)
         nc.sync.dma_start(out=list2[:], in_=offs2)
         nc.sync.dma_start(out=list3[:], in_=offs3)
         tab_w = [load_table(0, 2)]

from contextlib import ExitStack

import concourse.mybir as mybir

K, H, N, T, S, M, T2 = 1024, 1024, 512, 2048, 1024, 512, 1024
FLOPS = 2 * K * H * S + 2 * 2 * H * N * M

F32 = mybir.dt.float32
BF16 = mybir.dt.bfloat16
I32 = mybir.dt.int32
U32 = mybir.dt.uint32
U16 = mybir.dt.uint16
U8 = mybir.dt.uint8
FP8X4 = mybir.dt.float8_e4m3fn_x4
FP4X4 = mybir.dt.float4_e2m1fn_x4
ACT = mybir.ActivationFunctionType
ALU = mybir.AluOpType

P = 128
PACK = 4
KP = P * PACK
BANK = 512
LIST = 16


def tile_list_panel_disagreement_features_kernel(
    tc, tab_words, tab_scales, offs, w1, gain, offs2, wgt, context, wa_words, wa_scales, wb, offs3, wgo, out
):
    nc = tc.nc
    with ExitStack() as ctx:
        keep = ctx.enter_context(tc.tile_pool(name="keep", bufs=1))
        ring = ctx.enter_context(tc.tile_pool(name="ring", bufs=1))
        psum = ctx.enter_context(tc.psum_pool(name="psum", bufs=1))

        list1 = keep.tile([P, S // LIST], U16, name="list1")
        list2 = keep.tile([P, M // LIST], U16, name="list2")
        list3 = keep.tile([P, M // LIST], U16, name="list3")

        tab_sc = keep.tile([P, T], U8, name="tab_sc", align_bytes=64)
        nc.gpsimd.memset(tab_sc[:].bitcast(I32), 0)
        wa_sc = keep.tile([P, 2, N], U8, name="wa_sc", align_bytes=64)
        nc.gpsimd.memset(wa_sc[:].rearrange("p a c -> p (a c)").bitcast(I32), 0)
        pages = [keep.tile([P, T2], F32, name=f"page{i}") for i in range(PACK)]
        for page in pages:
            nc.vector.memset(page[:], 0.0)

        def load_rows(src, name, cuts=(0, PACK)):
            raw = ring.tile([P, PACK, BANK], F32, name=name, tag="raw", bufs=4)
            rows = src.rearrange("(p j) c -> p j c", j=PACK)
            for j0, j1 in zip(cuts, cuts[1:]):
                nc.sync.dma_start(out=raw[:, j0:j1, :], in_=rows[:, j0:j1, :])
            return raw

        def load_table(a, pieces=1):
            words = keep.tile([P, T], I32, name=f"tab_w{a}", align_bytes=64)
            src = tab_words[a].rearrange("p t i -> p (t i)").bitcast(I32)
            step = T // pieces
            for c in range(0, T, step):
                nc.sync.dma_start(out=words[:, c : c + step], in_=src[:, c : c + step])
            return words

        def load_context(b):
            rows = keep.tile([P, PACK, M], F32, name=f"ctx{b}")
            nc.sync.dma_start(out=rows[:], in_=context[b * KP : (b + 1) * KP, :].rearrange("(p t) m -> p t m", t=PACK))
            return rows

        nc.sync.dma_start(out=list1[:], in_=offs)
        gains = keep.tile([P, 2, PACK], F32, name="gains")
        nc.sync.dma_start(out=gains[:], in_=gain.rearrange("(b p t) -> p b t", b=2, t=PACK))
        warm = keep.tile([P, 1], F32, name="warm")
        nc.scalar.activation(out=warm[:], in_=gains[:, 0, 0:1], func=ACT.Abs_reciprocal_sqrt, bias=1.0)
        nc.sync.dma_start(out=list2[:], in_=offs2)
        nc.sync.dma_start(out=list3[:], in_=offs3)
        tab_w = [load_table(0, 2)]
        for q in range(4):
            nc.sync.dma_start(
                out=tab_sc[32 * q : 32 * q + 8, :].bitcast(I32),
                in_=tab_scales[:, 4 * q : 4 * q + 4, :].bitcast(I32),
            )
        w1_raw = {(0, 0): load_rows(w1[0:KP, 0:KP], "w1_raw00", (0, 1, 2, 4))}
        tab_w.append(load_table(1))
        w1_raw[1, 0] = load_rows(w1[KP : 2 * KP, 0:KP], "w1_raw10")
        wa_w = keep.tile([P, 2, 2 * N], U8, name="wa_w", align_bytes=64)
        nc.sync.dma_start(out=wa_w[:].bitcast(I32), in_=wa_words.rearrange("a p c -> p a c").bitcast(I32))
        for q in range(4):
            nc.sync.dma_start(
                out=wa_sc[32 * q : 32 * q + 4].bitcast(I32),
                in_=wa_scales[:, 4 * q : 4 * q + 4, :].rearrange("a r c -> r a c").bitcast(I32),
            )
        wgt_sb = keep.tile([P, M], F32, name="wgt_sb")
        nc.sync.dma_start(out=wgt_sb[:], in_=wgt)
        w1_raw[0, 1] = load_rows(w1[0:KP, KP : 2 * KP], "w1_raw01")
        w1_raw[1, 1] = load_rows(w1[KP : 2 * KP, KP : 2 * KP], "w1_raw11")
        ctx_sb = [load_context(0)]
        wb_raw = [load_rows(wb[b * KP : (b + 1) * KP, :], f"wb_raw{b}") for b in range(2)]
        ctx_sb.append(load_context(1))
        wgo_sb = keep.tile([P, M], F32, name="wgo_sb")
        nc.sync.dma_start(out=wgo_sb[:], in_=wgo)

        v_w = [keep.tile([P, S], U32, name="v_w0", align_bytes=64)]
        v_sc = keep.tile([P, S], U8, name="v_sc", align_bytes=64)
        nc.vector.tensor_copy(v_w[0][:], tab_w[0][:].bitcast(U32).indirect(list1[:]))
        nc.vector.tensor_copy(v_sc[:], tab_sc[:].indirect(list1[:]))

        def cast(on_vector, dst, src):
            if on_vector:
                nc.vector.tensor_copy(dst, src)
            else:
                nc.scalar.copy(dst, src)

        def quantize(grouped, name):
            width = grouped.shape[1] // PACK
            codes = keep.tile([P, width], U32, name=name + "_w", tag=name, align_bytes=64)
            scales = keep.tile([P, width], U8, name=name + "_sc", align_bytes=64)
            nc.vector.quantize_mx(out=codes[:].bitcast(FP8X4), scales=scales[:], in_=grouped)
            return codes, scales

        def group_w1(a, b, u, on_vector):
            tag = f"w1g{a}{u}" if b == 0 else f"h0{2 * u + a}"
            grouped = keep.tile([P, 2 * KP], BF16, name=f"w1g{a}{b}{u}", tag=tag, align_bytes=64)
            cast(
                on_vector,
                grouped[:].rearrange("p (e m j) -> p m j e", e=2, j=PACK),
                w1_raw[a, b][:].rearrange("p j (m t) -> p m j t", t=PACK)[:, :, :, 2 * u : 2 * u + 2],
            )
            return grouped[:]

        def group_wb(b, u, grouped):
            nc.scalar.activation(
                out=grouped.rearrange("p (e m j) -> p m j e", e=2, j=PACK),
                in_=wb_raw[b][:].rearrange("p j (m t) -> p m j t", t=PACK)[:, :, :, 2 * u : 2 * u + 2],
                func=ACT.Copy,
                scale=-1.0 if u == 0 else 1.0,
            )
            return grouped

        w1_q = {}

        def first_pass(a, b, t, half, bank):
            codes, scales = w1_q[a, b, t // 2]
            cols = slice((t % 2) * P, (t % 2 + 1) * P)
            picked = slice(half * BANK, (half + 1) * BANK)
            nc.tensor.matmul_mx(
                out=bank[:],
                lhsT=codes[:, cols].bitcast(FP8X4),
                lhsT_scale=scales[:, cols],
                rhs=v_w[a][:, picked].bitcast(FP8X4),
                rhs_scale=v_sc[4 * a :, picked],
                start=(a == 0),
                stop=(a == 1),
            )

        def new_bank(name, number):
            return psum.tile([P, BANK], F32, name=name, tag=f"bank{number}")

        def leave_h(b, t, banks):
            h = keep.tile([P, S], F32, name=f"h{b}{t}", tag=f"h{b}{t}", align_bytes=64)
            row_gain = gains[:, b, t : t + 1]
            for half in range(2):
                cols = slice(half * BANK, (half + 1) * BANK)
                if (b, t, half) == (0, 0, 1):
                    nc.vector.tensor_scalar(h[:, cols], banks[half][:], row_gain, None, ALU.mult)
                else:
                    nc.scalar.activation(out=h[:, cols], in_=banks[half][:], func=ACT.Copy, scale=row_gain)
            return h

        def pick(h, x, lo, hi):
            nc.vector.tensor_tensor(
                x, h[:].indirect(list2[:, lo // LIST : hi // LIST]), wgt_sb[:, lo:hi], ALU.mult
            )

        def add_context(b, x, lo, hi, tag):
            z = ring.tile([P, (hi - lo) * PACK], BF16, name=f"z{b}{lo}", tag=tag, align_bytes=64)
            nc.vector.tensor_tensor(
                z[:].rearrange("p (c i t) -> p c t i", i=2, t=PACK),
                x.rearrange("p t (c i) -> p c t i", i=2),
                ctx_sb[b][:, :, lo:hi].rearrange("p t (c i) -> p c t i", i=2),
                ALU.add,
            )
            return z[:]

        for u in range(2):
            w1_q[0, 0, u] = quantize(group_w1(0, 0, u, False), f"w1q00{u}")
        banks = {(t, half): new_bank(f"h0{t}{half}", 2 * t + half) for t in range(PACK) for half in range(2)}
        for t in range(PACK):
            for half in range(2):
                first_pass(0, 0, t, half, banks[t, half])
        v_w.append(keep.tile([P, S], U32, name="v_w1", tag="w1g01", align_bytes=64))
        nc.vector.tensor_copy(v_w[1][:], tab_w[1][:].bitcast(U32).indirect(list1[:]))
        for u in range(2):
            w1_q[1, 0, u] = quantize(group_w1(1, 0, u, u == 0), f"w1q10{u}")
        wa_pw = keep.tile([P, 2, N], U16, name="wa_pw", tag="w1g10", align_bytes=64)
        wa_psc = keep.tile([P, 2, N], U8, name="wa_psc", tag="w1g11", align_bytes=64)
        x0 = ring.tile([P, PACK, M], F32, name="x0")
        for t in range(PACK):
            for half in range(2):
                first_pass(1, 0, t, half, banks[t, half])
            pick(leave_h(0, t, [banks[t, 0], banks[t, 1]]), x0[:, t, :], 0, M)
            if t % 2 == 1:
                for a in range(2):
                    w1_q[a, 1, t // 2] = quantize(group_w1(a, 1, t // 2, t == 1 and a == 1), f"w1q{a}1{t // 2}")
        nc.vector.tensor_copy(
            wa_pw[:].rearrange("p a (i m) -> p a i m", i=PACK),
            wa_w[:].bitcast(U16).rearrange("p a (m i) -> p a i m", i=PACK),
        )
        nc.vector.tensor_copy(
            wa_psc[:].rearrange("p a (i m) -> p a i m", i=PACK),
            wa_sc[:].rearrange("p a (m i) -> p a i m", i=PACK),
        )

        half_m = M // 2
        z_q = {}
        wb_q = {}
        x1 = ring.tile([P, PACK, M], F32, name="x1")
        for t in range(PACK):
            pair = [new_bank(f"h1{t}{half}", 2 * t + half) for half in range(2)]
            for half in range(2):
                for a in range(2):
                    first_pass(a, 1, t, half, pair[half])
            h = leave_h(1, t, pair)
            if t < PACK - 1:
                pick(h, x1[:, t, :], 0, M)
            else:
                pick(h, x1[:, t, 0:half_m], 0, half_m)
            if t == 0:
                z_q[0, 0] = quantize(add_context(0, x0[:], 0, M, "za"), "zq0")
            if t < 2:
                tag = "h00" if t == 0 else "w1q010"
                grouped = keep.tile([P, 2 * KP], BF16, name=f"wbg{t}0", tag=tag, align_bytes=64)
                wb_q[t, 0] = quantize(group_wb(t, 0, grouped[:]), f"wbq{t}0")
        z_q[1, 0] = quantize(add_context(1, x1[:, :, 0:half_m], 0, half_m, "zb"), "zq10")
        pick(h, x1[:, PACK - 1, half_m:M], half_m, M)
        z_q[1, half_m] = quantize(add_context(1, x1[:, :, half_m:M], half_m, M, "zc"), "zq11")
        grouped = keep.tile([P, 2, 2 * KP], BF16, name="wbg1", tag="h12", align_bytes=64)
        for b in range(2):
            wb_q[b, 1] = quantize(group_wb(b, 1, grouped[:, b, :]), f"wbq{b}1")

        def second_pass(sums, weight, b, i, lo, hi, start, stop):
            cols = slice(i * P, (i + 1) * P)
            if weight == "a":
                lhs, lhs_scale = wa_pw[:, b, cols].bitcast(FP4X4), wa_psc[:, b, cols]
            else:
                codes, scales = wb_q[b, i // 2]
                cols = slice((i % 2) * P, (i % 2 + 1) * P)
                lhs, lhs_scale = codes[:, cols].bitcast(FP8X4), scales[:, cols]
            pieces = [(lo, hi)] if b == 0 else [(s, s + half_m) for s in range(lo, hi, half_m)]
            for n, (c0, c1) in enumerate(pieces):
                base = 0 if b == 0 else c0
                codes, scales = z_q[b, base]
                nc.tensor.matmul_mx(
                    out=sums[:, c0 - lo : c1 - lo], lhsT=lhs, lhsT_scale=lhs_scale,
                    rhs=codes[:, c0 - base : c1 - base].bitcast(FP8X4), rhs_scale=scales[:, c0 - base : c1 - base],
                    start=start and n == 0, stop=stop and n == len(pieces) - 1,
                )

        def work_tile(tag, name, width):
            return ring.tile([P, width], F32, name=f"{tag}{name}", tag=tag, bufs=2)[:]

        def root_of(first, name, width):
            size, root = work_tile("size", name, width), work_tile("root", name, width)
            nc.scalar.activation(out=size, in_=first, func=ACT.Abs)
            nc.scalar.activation(out=root, in_=size, func=ACT.Abs_reciprocal_sqrt, bias=1.0)
            return root

        out_rows = out.rearrange("(p i) c -> p i c", i=PACK)

        def put(i, y, lo, hi):
            nc.vector.tensor_tensor(
                pages[i][:].indirect(list3[:, lo // LIST : hi // LIST]), y, wgo_sb[:, lo:hi], ALU.mult
            )
            if hi == M:
                nc.sync.dma_start(out=out_rows[:, i, :], in_=pages[i][:])

        def finish_summed(i, first, diff, lo, hi):
            name, width = f"{i}_{lo}", hi - lo
            root = root_of(first, name, width)
            damp, square, y = (work_tile(tag, name, width) for tag in ("damp", "square", "y"))
            nc.scalar.activation(out=damp, in_=root, func=ACT.Square)
            nc.scalar.activation(out=square, in_=diff, func=ACT.Square)
            nc.vector.tensor_tensor(y, square, damp, ALU.mult)
            put(i, y, lo, hi)

        for half in range(2):
            lo, hi = half * half_m, (half + 1) * half_m
            bank = new_bank(f"o0{half}", half)
            first, diff = bank[:, 0:half_m], bank[:, half_m:M]
            for b in range(2):
                second_pass(first, "a", b, 0, lo, hi, b == 0, False)
                second_pass(diff, "a", b, 0, lo, hi, False, False)
                second_pass(diff, "b", b, 0, lo, hi, False, b == 1)
            finish_summed(0, first, diff, lo, hi)

        first, diff = new_bank("o1f", 2)[:], new_bank("o1d", 3)[:]
        for b in range(2):
            second_pass(first, "a", b, 1, 0, M, b == 0, b == 1)
            second_pass(diff, "a", b, 1, 0, M, b == 0, False)
            second_pass(diff, "b", b, 1, 0, M, False, b == 1)
        finish_summed(1, first, diff, 0, M)

        rel = {}
        for i in (2, 3):
            first, second = new_bank(f"o{i}f", 2 * i)[:], new_bank(f"o{i}s", 2 * i + 1)[:]
            for b in range(2):
                second_pass(second, "b", b, i, 0, M, b == 0, b == 1)
                second_pass(first, "a", b, i, 0, M, b == 0, b == 1)
            second_sb, diff, rel[i] = (work_tile(tag, i, M) for tag in ("second", "diff", "rel"))
            nc.scalar.copy(second_sb, second)
            root = root_of(first, i, M)
            nc.vector.tensor_tensor(diff, first, second_sb, ALU.subtract)
            nc.vector.tensor_tensor(rel[i], diff, root, ALU.mult)
        for i in (2, 3):
            y = work_tile("y", i, M)
            nc.scalar.activation(out=y, in_=rel[i], func=ACT.Square)
            put(i, y, 0, M)
